import numpy as np
import ml_dtypes


def mxq(x, axis, fmt="e4m3"):
    dtype, down = {"e4m3": (ml_dtypes.float8_e4m3fn, 7), "e5m2": (ml_dtypes.float8_e5m2, 14)}[fmt]
    v = np.moveaxis(np.asarray(x, np.float32).astype(ml_dtypes.bfloat16).astype(np.float64), axis, -1)
    blocks = v.reshape(v.shape[:-1] + (-1, 32))
    amax = np.abs(blocks).max(-1, keepdims=True)
    byte = np.maximum(np.where(amax > 0, np.frexp(amax)[1] - 1 + 127, 0) - down, 1)
    scale = np.exp2(byte - 127.0)
    codes = (blocks / scale).astype(np.float32).astype(dtype).astype(np.float64)
    return np.moveaxis((codes * scale).reshape(v.shape), -1, axis)


WIDE = False


def mx_kscale(k):
    if not WIDE:
        return np.ones(k)
    levels = np.array([10, -10, 5, -5, 0])
    if k % 512:
        return np.exp2(np.random.permutation(np.resize(levels, k // 32))).repeat(32)
    a = np.empty((k // 512, 16))
    for p in range(k // 512):
        a[p, :8] = np.random.permutation(np.resize(levels, 8))
        for g in range(8):
            far = levels[np.abs(levels - a[p, g]) >= 10]
            a[p, g + 8] = far[np.random.randint(len(far))]
    return np.exp2(a.ravel()).repeat(32)


def f64(x):
    return np.asarray(x).astype(np.float64)


def striped(idx):
    return np.tile(np.asarray(idx).reshape(-1, 16).T, (8, 1)).astype(np.uint16)


def unstriped(offs):
    return offs[:16].T.reshape(-1).astype(np.int64)


E2M1 = np.array([0.0, 0.5, 1.0, 1.5, 2.0, 3.0, 4.0, 6.0, -0.0, -0.5, -1.0, -1.5, -2.0, -3.0, -4.0, -6.0])


def pack_weight(w, fmt):
    k, n = w.shape
    w = f64(np.asarray(w, np.float32).astype(ml_dtypes.bfloat16)).reshape(k // 32, 32, n)
    amax = np.abs(w).max(1)
    if fmt == "e4m3":
        byte = np.frexp(amax)[1] - 1 + 127 - 7
    else:
        mant, ex = np.frexp(amax / 6.0)
        byte = np.where(mant > 0.5, ex, ex - 1) + 127
    byte = np.clip(np.where(amax > 0, byte, 1), 1, 254)
    scaled = (w * np.exp2(127.0 - byte)[:, None, :]).reshape(k, n).astype(np.float32)
    by_word = np.ascontiguousarray(scaled.reshape(k // 512, 128, 4, n).transpose(0, 1, 3, 2))
    if fmt == "e4m3":
        words = by_word.astype(ml_dtypes.float8_e4m3fn).view(np.uint8)
    else:
        c = by_word.astype(ml_dtypes.float4_e2m1fn).view(np.uint8) & 0xF
        words = (c[..., 0::2] | (c[..., 1::2] << 4)).reshape(k // 512, 128, 2 * n)
    return np.ascontiguousarray(words), np.ascontiguousarray(byte.astype(np.uint8).reshape(k // 512, 16, n))


def unpack_weight(words, scales, fmt):
    g, _, n = scales.shape
    words = np.ascontiguousarray(words).reshape(g, 128, n, -1)
    if fmt == "e4m3":
        vals = words.view(ml_dtypes.float8_e4m3fn).astype(np.float64)
    else:
        nib = np.empty((g, 128, n, 4), np.uint8)
        nib[..., 0::2] = words & 0xF
        nib[..., 1::2] = words >> 4
        vals = E2M1[nib]
    vals = vals * np.repeat(np.exp2(scales.astype(np.float64) - 127.0), 8, axis=1)[..., None]
    return vals.transpose(0, 1, 3, 2).reshape(g * 512, n)


D, T, I, Q, E, K = 512, 2048, 512, 128, 512, 16


def setup_inputs():
    n = np.random.standard_normal
    idx = np.random.permutation(T)[:I]
    idx2 = np.random.permutation(T)[:I]
    idx3 = np.random.permutation(T)[:I]
    fd = mx_kscale(D)
    fi = mx_kscale(I)
    ti = np.ones(T)
    ti[idx] = fi
    keysp = pack_weight(n((D, T)) / fd[:, None], "e4m3")
    return {
        "query": (n((D, Q)) * 1.0 / np.sqrt(D) * fd[:, None]).astype(np.float32),
        "keys_words": keysp[0],
        "keys_scales": keysp[1],
        "lam": (np.random.uniform(0.4, 1.0, (Q, 1))).astype(np.float32),
        "os": (np.random.uniform(4.0, 16.0, (1, I)) * fi).astype(np.float32),
        "vals": (n((E, T)) / ti).astype(np.float32),
        "before": (n((Q, E))).astype(np.float32),
        "hold": (np.random.uniform(0.1, 0.6, (Q, 1))).astype(np.float32),
        "offs": striped(idx),
        "offs2": striped(idx2),
        "offs3": striped(idx3),
    }


def reference(query, keys_words, keys_scales, lam, os, vals, before, hold, offs, offs2, offs3):
    idx = unstriped(offs)
    idx2 = unstriped(offs2)
    idx3 = unstriped(offs3)
    keysu = unpack_weight(keys_words, keys_scales, "e4m3")
    queryq = mxq(f64(query), 0, "e4m3")
    a = queryq.T @ keysu
    s = a[:, idx] + np.tanh(a[:, idx2] - a[:, idx3]) * f64(lam)
    p = np.exp(s - np.max(s, axis=1, keepdims=True))
    r = p / np.sum(p, axis=1, keepdims=True)
    rt = r.T
    rg = rt.reshape(I, K, Q // K).sum(axis=2)
    rq = 1.0 / np.sqrt(rg)
    rr = np.repeat(rq, Q // K, axis=1)
    w0 = rt * rr
    w = w0.T
    wo1 = w * f64(os)
    wt1 = wo1.T
    vt1 = f64(vals)[:, idx].T
    wt1q = mxq(wt1, 0, "e4m3")
    vt1q = mxq(vt1, 0, "e4m3")
    o = wt1q.T @ vt1q
    y = f64(before) * f64(hold) + o * (1.0 - f64(hold))
    return y

@@ -1,0 +1,215 @@
+from contextlib import ExitStack
+
+import concourse.mybir as mybir
+from concourse.masks import make_identity
+
+D, T, I, Q, E, K = 512, 2048, 512, 128, 512, 16
+FLOPS = 2 * Q * D * T + 2 * Q * I * E
+
+F32 = mybir.dt.float32
+BF16 = mybir.dt.bfloat16
+I32 = mybir.dt.int32
+U32 = mybir.dt.uint32
+U16 = mybir.dt.uint16
+U8 = mybir.dt.uint8
+FP8X4 = mybir.dt.float8_e4m3fn_x4
+ALU = mybir.AluOpType
+ACT = mybir.ActivationFunctionType
+AXIS = mybir.AxisListType
+
+P = 128
+PACK = 4
+BANK = 512
+GROUP = Q // K
+KEY_LOADS = ((0, 512), (512, 1024), (1024, 2048))
+SCORE_PIECES = ((0, 512), (512, 1024), (1024, 1536), (1536, 1792), (1792, 2048))
+OUT_HALF = E // 2
+
+
+def tile_attend_seconded_balanced_blend_kernel(tc, query, keys_words, keys_scales, lam, slot_factor, vals, before, hold, offs, offs2, offs3, out):
+    nc = tc.nc
+    with ExitStack() as ctx:
+        lists = ctx.enter_context(tc.tile_pool(name="lists", bufs=1))
+        keep = ctx.enter_context(tc.tile_pool(name="keep", bufs=1))
+        psum = ctx.enter_context(tc.psum_pool(name="psum", bufs=1))
+
+        def bank(b):
+            return psum.tile([P, BANK], F32, name="bank%d" % b, tag="bank%d" % b)
+
+        key_scales = keep.tile([P, BANK], U8, align_bytes=64)
+        nc.vector.memset(key_scales[:].bitcast(I32), 0)
+        one = keep.tile([P, 1], F32)
+        nc.vector.memset(one[:], 1.0)
+        huge = keep.tile([P, 1], F32, tag="huge", align_bytes=64)
+        nc.scalar.activation(huge[:], one[:], ACT.Copy, scale=2.0**96)
+
+        q_raw = keep.tile([P, PACK, Q], F32)
+        nc.sync.dma_start(out=q_raw[:], in_=query.rearrange("(p t) q -> p t q", t=PACK))
+        for quad in range(4):
+            rows = keys_scales[0, 4 * quad : 4 * quad + 4, :].bitcast(I32)
+            nc.sync.dma_start(
+                out=key_scales[32 * quad : 32 * quad + 16, :].bitcast(I32),
+                in_=rows.rearrange("r (j c) -> j r c", j=4),
+            )
+        key_rows = keys_words[0].rearrange("p n t -> p (n t)")
+        key_tiles = []
+        for n, (c0, c1) in enumerate(KEY_LOADS):
+            words = keep.tile([P, c1 - c0], U32, name="keys%d" % n, align_bytes=64)
+            nc.sync.dma_start(out=words[:].bitcast(I32), in_=key_rows[:, 4 * c0 : 4 * c1].bitcast(I32))
+            key_tiles.append(words)
+        own = lists.tile([P, I // 16], U16)
+        seconder = lists.tile([P, I // 16], U16)
+        opponent = lists.tile([P, I // 16], U16)
+        nc.sync.dma_start(opponent[:], offs3)
+        nc.sync.dma_start(seconder[:], offs2)
+        nc.sync.dma_start(own[:], offs)
+
+        val_tiles = [keep.tile([P, T], F32, name="vals%d" % j, tag="vals%d" % j, align_bytes=64) for j in range(4)]
+        lam_col = keep.tile([P, 1], F32)
+        hold_col = keep.tile([P, 1], F32)
+        os_cols = keep.tile([P, PACK], F32)
+        before_sb = keep.tile([P, E], F32)
+        nc.sync.dma_start(out=val_tiles[0][:], in_=vals[0:P, :])
+        nc.sync.dma_start(out=lam_col[:], in_=lam)
+        nc.sync.dma_start(out=before_sb[:], in_=before)
+        for j in range(1, 4):
+            nc.sync.dma_start(out=val_tiles[j][:], in_=vals[j * P : (j + 1) * P, :])
+        nc.sync.dma_start(out=os_cols[:], in_=slot_factor.rearrange("o (p t) -> (o p) t", t=PACK))
+        nc.gpsimd.dma_start(out=hold_col[:], in_=hold)
+        give = keep.tile([P, 1], F32)
+        nc.gpsimd.tensor_scalar(give[:], hold_col[:], -1.0, 1.0, ALU.mult, ALU.add)
+
+        ident = keep.tile([P, P], F32)
+        make_identity(nc, ident[:])
+
+        q_grouped = keep.tile([P, Q, PACK], BF16, align_bytes=64)
+        nc.vector.tensor_copy(out=q_grouped[:], in_=q_raw[:].rearrange("p t q -> p q t"))
+        q_codes = keep.tile([P, Q], U32, align_bytes=64)
+        q_scales = keep.tile([P, Q], U8, align_bytes=64)
+        nc.vector.quantize_mx(out=q_codes[:].bitcast(FP8X4), scales=q_scales[:], in_=q_grouped[:].rearrange("p q t -> p (q t)"))
+
+        scores = keep.tile([P, T], F32)
+        for n, (c0, c1) in enumerate(SCORE_PIECES):
+            load = [m for m, (l0, l1) in enumerate(KEY_LOADS) if l0 <= c0 < l1][0]
+            l0 = KEY_LOADS[load][0]
+            plane = c0 // BANK
+            acc = bank(n)
+            nc.tensor.matmul_mx(
+                out=acc[:, 0 : c1 - c0],
+                lhsT=q_codes[:].bitcast(FP8X4),
+                lhsT_scale=q_scales[:],
+                rhs=key_tiles[load][:, c0 - l0 : c1 - l0].bitcast(FP8X4),
+                rhs_scale=key_scales[4 * plane : P, c0 - BANK * plane : c1 - BANK * plane],
+                start=True,
+                stop=True,
+            )
+            if n % 2 == 0:
+                nc.vector.tensor_copy(out=scores[:, c0:c1], in_=acc[:, 0 : c1 - c0])
+            else:
+                nc.scalar.copy(out=scores[:, c0:c1], in_=acc[:, 0 : c1 - c0])
+
+        v_codes = keep.tile([P, E], U32, align_bytes=64)
+        v_scales = keep.tile([P, E], U8, align_bytes=64)
+
+        def gather_values(j, tag):
+            picked = keep.tile([P, I], BF16, name="picked%d" % j, tag=tag)
+            nc.vector.tensor_copy(out=picked[:], in_=val_tiles[j][:].indirect(own[:]))
+            pairs = picked[:].bitcast(F32)
+            turned = bank(j)
+            for u in range(2):
+                nc.tensor.transpose(turned[:, u * P : (u + 1) * P], pairs[:, u : 2 * P : 2], ident[:])
+            return turned
+
+        def interleave_values(turned, grouped):
+            nc.scalar.copy(
+                out=grouped.bitcast(F32).rearrange("p (e u) -> p e u", u=2),
+                in_=turned[:, 0 : 2 * P].rearrange("p (u e) -> p e u", u=2),
+            )
+
+        def quantize_values(j, grouped):
+            cols = slice(j * P, j * P + grouped.shape[1] // PACK)
+            nc.vector.quantize_mx(out=v_codes[:, cols].bitcast(FP8X4), scales=v_scales[:, cols], in_=grouped)
+
+        against = keep.tile([P, I], F32)
+        nc.vector.tensor_copy(out=against[:], in_=scores[:].indirect(opponent[:]))
+        turned0 = gather_values(0, "picked0")
+        grouped0 = keep.tile([P, P * PACK], BF16, align_bytes=64)
+        interleave_values(turned0, grouped0[:])
+        direct = keep.tile([P, I], F32, tag="direct")
+        nc.vector.tensor_copy(out=direct[:], in_=scores[:].indirect(own[:]))
+        margin = keep.tile([P, I], F32, tag="vals0", align_bytes=64)
+        nc.vector.tensor_tensor(margin[:], scores[:].indirect(seconder[:]), against[:], ALU.subtract)
+        vote = keep.tile([P, I], F32)
+        nc.scalar.activation(vote[:], margin[:], ACT.Tanh)
+        kept = keep.tile([P, E], F32)
+        nc.scalar.activation(kept[:], before_sb[:], ACT.Copy, scale=hold_col[:])
+        turned1 = gather_values(1, "picked1")
+        quantize_values(0, grouped0[:])
+        s = keep.tile([P, I], F32, tag="vals1", align_bytes=64)
+        nc.vector.scalar_tensor_tensor(s[:], vote[:], lam_col[:], direct[:], ALU.mult, ALU.add)
+        neg_max = keep.tile([P, 1], F32)
+        nc.vector.tensor_reduce(neg_max[:], s[:], AXIS.X, ALU.max, negate=True)
+        p_dealt = keep.tile([P, I], F32)
+        row_sum = keep.tile([P, 1], F32)
+        nc.scalar.activation(
+            p_dealt[:].rearrange("q (t s) -> q s t", t=PACK),
+            s[:].rearrange("q (s t) -> q s t", t=PACK),
+            ACT.Exp,
+            bias=neg_max[:],
+            accum_out=row_sum[:],
+        )
+        tiny = keep.tile([P, 1], F32)
+        nc.scalar.activation(tiny[:], row_sum[:], ACT.Abs_reciprocal_sqrt, bias=huge[:], scale=0.0)
+        turned2 = gather_values(2, "direct")
+        inv_sum = keep.tile([P, 1], F32, tag="vals2", align_bytes=64)
+        nc.vector.reciprocal(inv_sum[:], row_sum[:])
+        shares = keep.tile([P, I], F32)
+        nc.vector.tensor_scalar(shares[:], p_dealt[:], inv_sum[:], None, ALU.mult)
+        shares_t = bank(5)
+        for t in range(PACK):
+            nc.tensor.transpose(shares_t[:, t * P : (t + 1) * P], shares[:, t * P : (t + 1) * P], ident[:])
+        grouped12 = keep.tile([P, 2 * P * PACK], BF16, tag="huge", align_bytes=64)
+        interleave_values(turned1, grouped12[:, 0 : P * PACK])
+        interleave_values(turned2, grouped12[:, P * PACK : 2 * P * PACK])
+        turned3 = gather_values(3, "picked3")
+
+        group_sum = keep.tile([P, K, PACK], F32, tag="vals3", align_bytes=64)
+        nc.vector.tensor_reduce(
+            group_sum[:].rearrange("p k t -> p t k"),
+            shares_t[:].rearrange("p (t k j) -> p t k j", t=PACK, j=GROUP),
+            AXIS.X,
+            ALU.add,
+        )
+        inv_root = keep.tile([P, K, PACK], F32)
+        nc.scalar.activation(inv_root[:], group_sum[:], ACT.Abs_reciprocal_sqrt, bias=tiny[:], scale=2.0**40)
+        grouped3 = keep.tile([P, P * PACK], BF16, tag="vals3", align_bytes=64)
+        interleave_values(turned3, grouped3[:])
+        quantize_values(1, grouped12[:])
+        factor = keep.tile([P, K, PACK], F32)
+        nc.vector.scalar_tensor_tensor(factor[:], inv_root[:], 2.0**20, os_cols[:].unsqueeze(1).to_broadcast([P, K, PACK]), ALU.mult, ALU.mult)
+        w_grouped = keep.tile([P, Q * PACK], BF16, align_bytes=64)
+        nc.vector.tensor_tensor(
+            w_grouped[:].rearrange("p (k j t) -> p k j t", j=GROUP, t=PACK),
+            shares_t[:].rearrange("p (t k j) -> p k j t", t=PACK, j=GROUP),
+            factor[:].unsqueeze(2).to_broadcast([P, K, GROUP, PACK]),
+            ALU.mult,
+        )
+        quantize_values(3, grouped3[:])
+        w_codes = keep.tile([P, Q], U32, align_bytes=64)
+        w_scales = keep.tile([P, Q], U8, align_bytes=64)
+        nc.vector.quantize_mx(out=w_codes[:].bitcast(FP8X4), scales=w_scales[:], in_=w_grouped[:])
+        for h in range(2):
+            cols = slice(h * OUT_HALF, (h + 1) * OUT_HALF)
+            acc = bank(6 + h)
+            nc.tensor.matmul_mx(
+                out=acc[:, 0:OUT_HALF],
+                lhsT=w_codes[:].bitcast(FP8X4),
+                lhsT_scale=w_scales[:],
+                rhs=v_codes[:, cols].bitcast(FP8X4),
+                rhs_scale=v_scales[:, cols],
+                start=True,
+                stop=True,
+            )
+            result = keep.tile([P, OUT_HALF], F32, name="result%d" % h)
+            nc.vector.scalar_tensor_tensor(result[:], acc[:, 0:OUT_HALF], give[:], kept[:, cols], ALU.mult, ALU.add)
+            (nc.sync if h == 0 else nc.scalar).dma_start(out=out[:, cols], in_=result[:])

@@ -108,17 +108,17 @@ def tile_attend_seconded_balanced_blend_kernel(tc, query, keys_words, keys_scale
             else:
                 nc.scalar.copy(out=scores[:, c0:c1], in_=acc[:, 0 : c1 - c0])
 
-        v_codes = keep.tile([P, E], U32, align_bytes=64)
-        v_scales = keep.tile([P, E], U8, align_bytes=64)
-
-        def gather_values(j, tag):
-            picked = keep.tile([P, I], BF16, name="picked%d" % j, tag=tag)
-            nc.vector.tensor_copy(out=picked[:], in_=val_tiles[j][:].indirect(own[:]))
+        def turn_values(j, picked):
             pairs = picked[:].bitcast(F32)
             turned = bank(j)
             for u in range(2):
                 nc.tensor.transpose(turned[:, u * P : (u + 1) * P], pairs[:, u : 2 * P : 2], ident[:])
             return turned
+
+        def gather_values(j, tag):
+            picked = keep.tile([P, I], BF16, name="picked%d" % j, tag=tag)
+            nc.vector.tensor_copy(out=picked[:], in_=val_tiles[j][:].indirect(own[:]))
+            return turn_values(j, picked)
 
         def interleave_values(turned, grouped):
             nc.scalar.copy(
@@ -126,31 +126,35 @@ def tile_attend_seconded_balanced_blend_kernel(tc, query, keys_words, keys_scale
                 in_=turned[:, 0 : 2 * P].rearrange("p (u e) -> p e u", u=2),
             )
 
-        def quantize_values(j, grouped):
-            cols = slice(j * P, j * P + grouped.shape[1] // PACK)
-            nc.vector.quantize_mx(out=v_codes[:, cols].bitcast(FP8X4), scales=v_scales[:, cols], in_=grouped)
+        rounded = keep.tile([P, T], BF16, tag="rounded")
+        for c0 in range(0, T, BANK):
+            nc.scalar.copy(out=rounded[:, c0 : c0 + BANK], in_=val_tiles[0][:, c0 : c0 + BANK])
+        picked0 = keep.tile([P, I], BF16)
+        half = I // 2
+        nc.scalar.activation(picked0[:, 0:half], rounded[:].indirect(own[:, 0 : half // 16]), ACT.Copy)
 
         against = keep.tile([P, I], F32)
-        nc.vector.tensor_copy(out=against[:], in_=scores[:].indirect(opponent[:]))
-        turned0 = gather_values(0, "picked0")
-        grouped0 = keep.tile([P, P * PACK], BF16, align_bytes=64)
-        interleave_values(turned0, grouped0[:])
+        margin = keep.tile([P, I], F32)
+        for h in range(2):
+            w = I // 2
+            nc.vector.tensor_copy(out=against[:, h * w : (h + 1) * w], in_=scores[:].indirect(opponent[:, h * w // 16 : (h + 1) * w // 16]))
+        for h in range(2):
+            w = I // 2
+            nc.vector.tensor_tensor(margin[:, h * w : (h + 1) * w], scores[:].indirect(seconder[:, h * w // 16 : (h + 1) * w // 16]), against[:, h * w : (h + 1) * w], ALU.subtract)
         direct = keep.tile([P, I], F32, tag="direct")
         nc.vector.tensor_copy(out=direct[:], in_=scores[:].indirect(own[:]))
-        margin = keep.tile([P, I], F32, tag="vals0", align_bytes=64)
-        nc.vector.tensor_tensor(margin[:], scores[:].indirect(seconder[:]), against[:], ALU.subtract)
-        vote = keep.tile([P, I], F32)
+        vote = keep.tile([P, I], F32, tag="vals0", align_bytes=64)
         nc.scalar.activation(vote[:], margin[:], ACT.Tanh)
-        kept = keep.tile([P, E], F32)
+        nc.scalar.activation(picked0[:, half:I], rounded[:].indirect(own[:, half // 16 : I // 16]), ACT.Copy)
+        turned0 = turn_values(0, picked0)
+        kept = keep.tile([P, E], F32, tag="rounded")
         nc.scalar.activation(kept[:], before_sb[:], ACT.Copy, scale=hold_col[:])
-        turned1 = gather_values(1, "picked1")
-        quantize_values(0, grouped0[:])
-        s = keep.tile([P, I], F32, tag="vals1", align_bytes=64)
+        s = keep.tile([P, I], F32)
         nc.vector.scalar_tensor_tensor(s[:], vote[:], lam_col[:], direct[:], ALU.mult, ALU.add)
         neg_max = keep.tile([P, 1], F32)
         nc.vector.tensor_reduce(neg_max[:], s[:], AXIS.X, ALU.max, negate=True)
-        p_dealt = keep.tile([P, I], F32)
-        row_sum = keep.tile([P, 1], F32)
+        p_dealt = keep.tile([P, I], F32, tag="p_dealt")
+        row_sum = keep.tile([P, 1], F32, tag="row_sum")
         nc.scalar.activation(
             p_dealt[:].rearrange("q (t s) -> q s t", t=PACK),
             s[:].rearrange("q (s t) -> q s t", t=PACK),
@@ -158,22 +162,22 @@ def tile_attend_seconded_balanced_blend_kernel(tc, query, keys_words, keys_scale
             bias=neg_max[:],
             accum_out=row_sum[:],
         )
-        tiny = keep.tile([P, 1], F32)
-        nc.scalar.activation(tiny[:], row_sum[:], ACT.Abs_reciprocal_sqrt, bias=huge[:], scale=0.0)
-        turned2 = gather_values(2, "direct")
-        inv_sum = keep.tile([P, 1], F32, tag="vals2", align_bytes=64)
+        tiny = keep.tile([P, 1], F32, tag="tiny", align_bytes=64)
+        nc.scalar.activation(tiny[:], p_dealt[:, 0:1], ACT.Abs_reciprocal_sqrt, bias=huge[:], scale=0.0)
+        turned1 = gather_values(1, "direct")
+        inv_sum = keep.tile([P, 1], F32)
         nc.vector.reciprocal(inv_sum[:], row_sum[:])
-        shares = keep.tile([P, I], F32)
+        shares = keep.tile([P, I], F32, tag="shares")
         nc.vector.tensor_scalar(shares[:], p_dealt[:], inv_sum[:], None, ALU.mult)
         shares_t = bank(5)
         for t in range(PACK):
             nc.tensor.transpose(shares_t[:, t * P : (t + 1) * P], shares[:, t * P : (t + 1) * P], ident[:])
-        grouped12 = keep.tile([P, 2 * P * PACK], BF16, tag="huge", align_bytes=64)
-        interleave_values(turned1, grouped12[:, 0 : P * PACK])
-        interleave_values(turned2, grouped12[:, P * PACK : 2 * P * PACK])
-        turned3 = gather_values(3, "picked3")
+        grouped01 = keep.tile([P, 2 * P * PACK], BF16, tag="huge", align_bytes=64)
+        interleave_values(turned0, grouped01[:, 0 : P * PACK])
+        interleave_values(turned1, grouped01[:, P * PACK : 2 * P * PACK])
+        turned2 = gather_values(2, "row_sum")
 
-        group_sum = keep.tile([P, K, PACK], F32, tag="vals3", align_bytes=64)
+        group_sum = keep.tile([P, K, PACK], F32, tag="group_sum", align_bytes=64)
         nc.vector.tensor_reduce(
             group_sum[:].rearrange("p k t -> p t k"),
             shares_t[:].rearrange("p (t k j) -> p t k j", t=PACK, j=GROUP),
@@ -182,11 +186,22 @@ def tile_attend_seconded_balanced_blend_kernel(tc, query, keys_words, keys_scale
         )
         inv_root = keep.tile([P, K, PACK], F32)
         nc.scalar.activation(inv_root[:], group_sum[:], ACT.Abs_reciprocal_sqrt, bias=tiny[:], scale=2.0**40)
-        grouped3 = keep.tile([P, P * PACK], BF16, tag="vals3", align_bytes=64)
+        grouped2 = keep.tile([P, P * PACK], BF16, tag="group_sum", align_bytes=64)
+        interleave_values(turned2, grouped2[:])
+        turned3 = gather_values(3, "shares")
+        grouped3 = keep.tile([P, P * PACK], BF16, align_bytes=64)
         interleave_values(turned3, grouped3[:])
-        quantize_values(1, grouped12[:])
         factor = keep.tile([P, K, PACK], F32)
         nc.vector.scalar_tensor_tensor(factor[:], inv_root[:], 2.0**20, os_cols[:].unsqueeze(1).to_broadcast([P, K, PACK]), ALU.mult, ALU.mult)
+
+        v_codes = keep.tile([P, E], U32, tag="tiny", align_bytes=64)
+        v_scales = keep.tile([P, E], U8, align_bytes=64)
+
+        def quantize_values(j, grouped):
+            cols = slice(j * P, j * P + grouped.shape[1] // PACK)
+            nc.vector.quantize_mx(out=v_codes[:, cols].bitcast(FP8X4), scales=v_scales[:, cols], in_=grouped)
+
+        quantize_values(0, grouped01[:])
         w_grouped = keep.tile([P, Q * PACK], BF16, align_bytes=64)
         nc.vector.tensor_tensor(
             w_grouped[:].rearrange("p (k j t) -> p k j t", j=GROUP, t=PACK),
@@ -194,15 +209,17 @@ def tile_attend_seconded_balanced_blend_kernel(tc, query, keys_words, keys_scale
             factor[:].unsqueeze(2).to_broadcast([P, K, GROUP, PACK]),
             ALU.mult,
         )
-        quantize_values(3, grouped3[:])
+        quantize_values(2, grouped2[:])
         w_codes = keep.tile([P, Q], U32, align_bytes=64)
         w_scales = keep.tile([P, Q], U8, align_bytes=64)
         nc.vector.quantize_mx(out=w_codes[:].bitcast(FP8X4), scales=w_scales[:], in_=w_grouped[:])
-        for h in range(2):
-            cols = slice(h * OUT_HALF, (h + 1) * OUT_HALF)
-            acc = bank(6 + h)
+        quantize_values(3, grouped3[:])
+
+        for n, (c0, c1) in enumerate(((0, 256), (256, 384), (384, 512))):
+            cols = slice(c0, c1)
+            acc = bank((6, 7, 4, 3)[n])
             nc.tensor.matmul_mx(
-                out=acc[:, 0:OUT_HALF],
+                out=acc[:, 0 : c1 - c0],
                 lhsT=w_codes[:].bitcast(FP8X4),
                 lhsT_scale=w_scales[:],
                 rhs=v_codes[:, cols].bitcast(FP8X4),
@@ -210,6 +227,6 @@ def tile_attend_seconded_balanced_blend_kernel(tc, query, keys_words, keys_scale
                 start=True,
                 stop=True,
             )
-            result = keep.tile([P, OUT_HALF], F32, name="result%d" % h)
-            nc.vector.scalar_tensor_tensor(result[:], acc[:, 0:OUT_HALF], give[:], kept[:, cols], ALU.mult, ALU.add)
-            (nc.sync if h == 0 else nc.scalar).dma_start(out=out[:, cols], in_=result[:])
+            result = keep.tile([P, c1 - c0], F32, name="result%d" % n)
+            nc.vector.scalar_tensor_tensor(result[:], acc[:, 0 : c1 - c0], give[:], kept[:, cols], ALU.mult, ALU.add)
+            (nc.sync if n % 2 == 0 else nc.scalar).dma_start(out=out[:, cols], in_=result[:])

@@ -60,17 +60,17 @@ def tile_attend_seconded_balanced_blend_kernel(tc, query, keys_words, keys_scale
         own = lists.tile([P, I // 16], U16)
         seconder = lists.tile([P, I // 16], U16)
         opponent = lists.tile([P, I // 16], U16)
-        nc.sync.dma_start(opponent[:], offs3)
-        nc.sync.dma_start(seconder[:], offs2)
-        nc.sync.dma_start(own[:], offs)
-
         val_tiles = [keep.tile([P, T], F32, name="vals%d" % j, tag="vals%d" % j, align_bytes=64) for j in range(4)]
         lam_col = keep.tile([P, 1], F32)
         hold_col = keep.tile([P, 1], F32)
         os_cols = keep.tile([P, PACK], F32)
         before_sb = keep.tile([P, E], F32)
-        nc.sync.dma_start(out=val_tiles[0][:], in_=vals[0:P, :])
-        nc.sync.dma_start(out=lam_col[:], in_=lam)
+        nc.sync.dma_start(out=val_tiles[0][:, 0 : T // 2], in_=vals[0:P, 0 : T // 2])
+        nc.sync.dma_start(opponent[:], offs3)
+        nc.sync.dma_start(seconder[:], offs2)
+        nc.sync.dma_start(own[:], offs)
+        nc.sync.dma_start(out=val_tiles[0][:, T // 2 : T], in_=vals[0:P, T // 2 : T])
+        nc.gpsimd.dma_start(out=lam_col[:], in_=lam)
         nc.sync.dma_start(out=before_sb[:], in_=before)
         for j in range(1, 4):
             nc.sync.dma_start(out=val_tiles[j][:], in_=vals[j * P : (j + 1) * P, :])
@@ -103,7 +103,7 @@ def tile_attend_seconded_balanced_blend_kernel(tc, query, keys_words, keys_scale
                 start=True,
                 stop=True,
             )
-            if n % 2 == 0:
+            if n != 1:
                 nc.vector.tensor_copy(out=scores[:, c0:c1], in_=acc[:, 0 : c1 - c0])
             else:
                 nc.scalar.copy(out=scores[:, c0:c1], in_=acc[:, 0 : c1 - c0])
@@ -127,8 +127,8 @@ def tile_attend_seconded_balanced_blend_kernel(tc, query, keys_words, keys_scale
             )
 
         rounded = keep.tile([P, T], BF16, tag="rounded")
-        for c0 in range(0, T, BANK):
-            nc.scalar.copy(out=rounded[:, c0 : c0 + BANK], in_=val_tiles[0][:, c0 : c0 + BANK])
+        for c0 in range(0, T, T // 2):
+            nc.scalar.copy(out=rounded[:, c0 : c0 + T // 2], in_=val_tiles[0][:, c0 : c0 + T // 2])
         picked0 = keep.tile([P, I], BF16)
         half = I // 2
         nc.scalar.activation(picked0[:, 0:half], rounded[:].indirect(own[:, 0 : half // 16]), ACT.Copy)

@@ -21,9 +21,23 @@ P = 128
 PACK = 4
 BANK = 512
 GROUP = Q // K
+LIST_ROWS = 16
+QUADRANTS = 4
+VALUE_TILES = E // P
+ALIGN = 64
+
 KEY_LOADS = ((0, 512), (512, 1024), (1024, 2048))
 SCORE_PIECES = ((0, 512), (512, 1024), (1024, 1536), (1536, 1792), (1792, 2048))
-OUT_HALF = E // 2
+SCALAR_SCORE_PIECE = 1
+OUT_PIECES = ((0, 256), (256, 384), (384, 512))
+SHARES_BANK = 5
+OUT_BANKS = (6, 7, 4)
+SLOT_HALVES = ((0, I // 2), (I // 2, I))
+TOKEN_HALVES = ((0, T // 2), (T // 2, T))
+
+ROOT_SCALE = 2.0**40
+ROOT_UNDO = 2.0**20
+GUARD_INVERSE_SQUARE = 2.0**96
 
 
 def tile_attend_seconded_balanced_blend_kernel(tc, query, keys_words, keys_scales, lam, slot_factor, vals, before, hold, offs, offs2, offs3, out):
@@ -36,74 +50,80 @@ def tile_attend_seconded_balanced_blend_kernel(tc, query, keys_words, keys_scale
         def bank(b):
             return psum.tile([P, BANK], F32, name="bank%d" % b, tag="bank%d" % b)
 
-        key_scales = keep.tile([P, BANK], U8, align_bytes=64)
+        def entries(list_tile, first, last):
+            return list_tile[:, first // LIST_ROWS : last // LIST_ROWS]
+
+        key_scales = keep.tile([P, BANK], U8, align_bytes=ALIGN)
         nc.vector.memset(key_scales[:].bitcast(I32), 0)
         one = keep.tile([P, 1], F32)
         nc.vector.memset(one[:], 1.0)
-        huge = keep.tile([P, 1], F32, tag="huge", align_bytes=64)
-        nc.scalar.activation(huge[:], one[:], ACT.Copy, scale=2.0**96)
+        guard_source = keep.tile([P, 1], F32, tag="guard_source", align_bytes=ALIGN)
+        nc.scalar.activation(guard_source[:], one[:], ACT.Copy, scale=GUARD_INVERSE_SQUARE)
 
         q_raw = keep.tile([P, PACK, Q], F32)
         nc.sync.dma_start(out=q_raw[:], in_=query.rearrange("(p t) q -> p t q", t=PACK))
-        for quad in range(4):
+        for quad in range(QUADRANTS):
             rows = keys_scales[0, 4 * quad : 4 * quad + 4, :].bitcast(I32)
             nc.sync.dma_start(
                 out=key_scales[32 * quad : 32 * quad + 16, :].bitcast(I32),
-                in_=rows.rearrange("r (j c) -> j r c", j=4),
+                in_=rows.rearrange("r (j c) -> j r c", j=T // BANK),
             )
         key_rows = keys_words[0].rearrange("p n t -> p (n t)")
         key_tiles = []
         for n, (c0, c1) in enumerate(KEY_LOADS):
-            words = keep.tile([P, c1 - c0], U32, name="keys%d" % n, align_bytes=64)
-            nc.sync.dma_start(out=words[:].bitcast(I32), in_=key_rows[:, 4 * c0 : 4 * c1].bitcast(I32))
+            words = keep.tile([P, c1 - c0], U32, name="keys%d" % n, align_bytes=ALIGN)
+            nc.sync.dma_start(out=words[:].bitcast(I32), in_=key_rows[:, PACK * c0 : PACK * c1].bitcast(I32))
             key_tiles.append(words)
-        own = lists.tile([P, I // 16], U16)
-        seconder = lists.tile([P, I // 16], U16)
-        opponent = lists.tile([P, I // 16], U16)
-        val_tiles = [keep.tile([P, T], F32, name="vals%d" % j, tag="vals%d" % j, align_bytes=64) for j in range(4)]
+        own = lists.tile([P, I // LIST_ROWS], U16)
+        seconder = lists.tile([P, I // LIST_ROWS], U16)
+        opponent = lists.tile([P, I // LIST_ROWS], U16)
+        val_tiles = [keep.tile([P, T], F32, name="vals%d" % j, tag="vals%d" % j, align_bytes=ALIGN) for j in range(VALUE_TILES)]
         lam_col = keep.tile([P, 1], F32)
-        hold_col = keep.tile([P, 1], F32)
-        os_cols = keep.tile([P, PACK], F32)
+        hold_col = keep.tile([P, 1], F32, tag="group_sum", align_bytes=ALIGN)
+        factor_cols = keep.tile([P, PACK], F32)
         before_sb = keep.tile([P, E], F32)
         nc.sync.dma_start(out=val_tiles[0][:, 0 : T // 2], in_=vals[0:P, 0 : T // 2])
         nc.sync.dma_start(opponent[:], offs3)
         nc.sync.dma_start(seconder[:], offs2)
         nc.sync.dma_start(own[:], offs)
         nc.sync.dma_start(out=val_tiles[0][:, T // 2 : T], in_=vals[0:P, T // 2 : T])
-        nc.gpsimd.dma_start(out=lam_col[:], in_=lam)
         nc.sync.dma_start(out=before_sb[:], in_=before)
-        for j in range(1, 4):
-            nc.sync.dma_start(out=val_tiles[j][:], in_=vals[j * P : (j + 1) * P, :])
-        nc.sync.dma_start(out=os_cols[:], in_=slot_factor.rearrange("o (p t) -> (o p) t", t=PACK))
-        nc.gpsimd.dma_start(out=hold_col[:], in_=hold)
+        nc.sync.dma_start(out=val_tiles[1][:], in_=vals[P : 2 * P, :])
+        nc.sync.dma_start(out=lam_col[:], in_=lam)
+        nc.sync.dma_start(out=val_tiles[2][:], in_=vals[2 * P : 3 * P, :])
+        nc.sync.dma_start(out=hold_col[:], in_=hold)
+        nc.sync.dma_start(out=val_tiles[3][:], in_=vals[3 * P : 4 * P, :])
+        nc.sync.dma_start(out=factor_cols[:], in_=slot_factor.rearrange("o (p t) -> (o p) t", t=PACK))
         give = keep.tile([P, 1], F32)
         nc.gpsimd.tensor_scalar(give[:], hold_col[:], -1.0, 1.0, ALU.mult, ALU.add)
+        stay = keep.tile([P, 1], F32)
+        nc.gpsimd.tensor_copy(out=stay[:], in_=hold_col[:])
 
         ident = keep.tile([P, P], F32)
         make_identity(nc, ident[:])
 
-        q_grouped = keep.tile([P, Q, PACK], BF16, align_bytes=64)
+        q_grouped = keep.tile([P, Q, PACK], BF16, align_bytes=ALIGN)
         nc.vector.tensor_copy(out=q_grouped[:], in_=q_raw[:].rearrange("p t q -> p q t"))
-        q_codes = keep.tile([P, Q], U32, align_bytes=64)
-        q_scales = keep.tile([P, Q], U8, align_bytes=64)
+        q_codes = keep.tile([P, Q], U32, align_bytes=ALIGN)
+        q_scales = keep.tile([P, Q], U8, align_bytes=ALIGN)
         nc.vector.quantize_mx(out=q_codes[:].bitcast(FP8X4), scales=q_scales[:], in_=q_grouped[:].rearrange("p q t -> p (q t)"))
 
         scores = keep.tile([P, T], F32)
         for n, (c0, c1) in enumerate(SCORE_PIECES):
             load = [m for m, (l0, l1) in enumerate(KEY_LOADS) if l0 <= c0 < l1][0]
-            l0 = KEY_LOADS[load][0]
+            first = KEY_LOADS[load][0]
             plane = c0 // BANK
             acc = bank(n)
             nc.tensor.matmul_mx(
                 out=acc[:, 0 : c1 - c0],
                 lhsT=q_codes[:].bitcast(FP8X4),
                 lhsT_scale=q_scales[:],
-                rhs=key_tiles[load][:, c0 - l0 : c1 - l0].bitcast(FP8X4),
+                rhs=key_tiles[load][:, c0 - first : c1 - first].bitcast(FP8X4),
                 rhs_scale=key_scales[4 * plane : P, c0 - BANK * plane : c1 - BANK * plane],
                 start=True,
                 stop=True,
             )
-            if n != 1:
+            if n != SCALAR_SCORE_PIECE:
                 nc.vector.tensor_copy(out=scores[:, c0:c1], in_=acc[:, 0 : c1 - c0])
             else:
                 nc.scalar.copy(out=scores[:, c0:c1], in_=acc[:, 0 : c1 - c0])
@@ -127,57 +147,58 @@ def tile_attend_seconded_balanced_blend_kernel(tc, query, keys_words, keys_scale
             )
 
         rounded = keep.tile([P, T], BF16, tag="rounded")
-        for c0 in range(0, T, T // 2):
-            nc.scalar.copy(out=rounded[:, c0 : c0 + T // 2], in_=val_tiles[0][:, c0 : c0 + T // 2])
+        for c0, c1 in TOKEN_HALVES:
+            nc.scalar.copy(out=rounded[:, c0:c1], in_=val_tiles[0][:, c0:c1])
         picked0 = keep.tile([P, I], BF16)
         half = I // 2
-        nc.scalar.activation(picked0[:, 0:half], rounded[:].indirect(own[:, 0 : half // 16]), ACT.Copy)
+        nc.scalar.activation(picked0[:, 0:half], rounded[:].indirect(entries(own, 0, half)), ACT.Copy)
 
         against = keep.tile([P, I], F32)
         margin = keep.tile([P, I], F32)
-        for h in range(2):
-            w = I // 2
-            nc.vector.tensor_copy(out=against[:, h * w : (h + 1) * w], in_=scores[:].indirect(opponent[:, h * w // 16 : (h + 1) * w // 16]))
-        for h in range(2):
-            w = I // 2
-            nc.vector.tensor_tensor(margin[:, h * w : (h + 1) * w], scores[:].indirect(seconder[:, h * w // 16 : (h + 1) * w // 16]), against[:, h * w : (h + 1) * w], ALU.subtract)
+        for i0, i1 in SLOT_HALVES:
+            nc.vector.tensor_copy(out=against[:, i0:i1], in_=scores[:].indirect(entries(opponent, i0, i1)))
+        for i0, i1 in SLOT_HALVES:
+            nc.vector.tensor_tensor(margin[:, i0:i1], scores[:].indirect(entries(seconder, i0, i1)), against[:, i0:i1], ALU.subtract)
         direct = keep.tile([P, I], F32, tag="direct")
-        nc.vector.tensor_copy(out=direct[:], in_=scores[:].indirect(own[:]))
-        vote = keep.tile([P, I], F32, tag="vals0", align_bytes=64)
+        for i0, i1 in SLOT_HALVES:
+            nc.vector.tensor_copy(out=direct[:, i0:i1], in_=scores[:].indirect(entries(own, i0, i1)))
+        vote = keep.tile([P, I], F32, tag="vals0", align_bytes=ALIGN)
         nc.scalar.activation(vote[:], margin[:], ACT.Tanh)
-        nc.scalar.activation(picked0[:, half:I], rounded[:].indirect(own[:, half // 16 : I // 16]), ACT.Copy)
+        nc.scalar.activation(picked0[:, half:I], rounded[:].indirect(entries(own, half, I)), ACT.Copy)
         turned0 = turn_values(0, picked0)
         kept = keep.tile([P, E], F32, tag="rounded")
-        nc.scalar.activation(kept[:], before_sb[:], ACT.Copy, scale=hold_col[:])
+        nc.scalar.activation(kept[:], before_sb[:], ACT.Copy, scale=stay[:])
         s = keep.tile([P, I], F32)
-        nc.vector.scalar_tensor_tensor(s[:], vote[:], lam_col[:], direct[:], ALU.mult, ALU.add)
+        for i0, i1 in SLOT_HALVES:
+            nc.vector.scalar_tensor_tensor(s[:, i0:i1], vote[:, i0:i1], lam_col[:], direct[:, i0:i1], ALU.mult, ALU.add)
+
         neg_max = keep.tile([P, 1], F32)
         nc.vector.tensor_reduce(neg_max[:], s[:], AXIS.X, ALU.max, negate=True)
         p_dealt = keep.tile([P, I], F32, tag="p_dealt")
         row_sum = keep.tile([P, 1], F32, tag="row_sum")
         nc.scalar.activation(
-            p_dealt[:].rearrange("q (t s) -> q s t", t=PACK),
-            s[:].rearrange("q (s t) -> q s t", t=PACK),
+            p_dealt[:].rearrange("q (t m) -> q m t", t=PACK),
+            s[:].rearrange("q (m t) -> q m t", t=PACK),
             ACT.Exp,
             bias=neg_max[:],
             accum_out=row_sum[:],
         )
-        tiny = keep.tile([P, 1], F32, tag="tiny", align_bytes=64)
-        nc.scalar.activation(tiny[:], p_dealt[:, 0:1], ACT.Abs_reciprocal_sqrt, bias=huge[:], scale=0.0)
+        guard = keep.tile([P, 1], F32, tag="guard", align_bytes=ALIGN)
+        nc.scalar.activation(guard[:], p_dealt[:, 0:1], ACT.Abs_reciprocal_sqrt, bias=guard_source[:], scale=0.0)
         turned1 = gather_values(1, "direct")
         inv_sum = keep.tile([P, 1], F32)
         nc.vector.reciprocal(inv_sum[:], row_sum[:])
         shares = keep.tile([P, I], F32, tag="shares")
         nc.vector.tensor_scalar(shares[:], p_dealt[:], inv_sum[:], None, ALU.mult)
-        shares_t = bank(5)
+        shares_t = bank(SHARES_BANK)
         for t in range(PACK):
             nc.tensor.transpose(shares_t[:, t * P : (t + 1) * P], shares[:, t * P : (t + 1) * P], ident[:])
-        grouped01 = keep.tile([P, 2 * P * PACK], BF16, tag="huge", align_bytes=64)
+        grouped01 = keep.tile([P, 2 * P * PACK], BF16, tag="guard_source", align_bytes=ALIGN)
         interleave_values(turned0, grouped01[:, 0 : P * PACK])
         interleave_values(turned1, grouped01[:, P * PACK : 2 * P * PACK])
         turned2 = gather_values(2, "row_sum")
 
-        group_sum = keep.tile([P, K, PACK], F32, tag="group_sum", align_bytes=64)
+        group_sum = keep.tile([P, K, PACK], F32, tag="group_sum", align_bytes=ALIGN)
         nc.vector.tensor_reduce(
             group_sum[:].rearrange("p k t -> p t k"),
             shares_t[:].rearrange("p (t k j) -> p t k j", t=PACK, j=GROUP),
@@ -185,39 +206,41 @@ def tile_attend_seconded_balanced_blend_kernel(tc, query, keys_words, keys_scale
             ALU.add,
         )
         inv_root = keep.tile([P, K, PACK], F32)
-        nc.scalar.activation(inv_root[:], group_sum[:], ACT.Abs_reciprocal_sqrt, bias=tiny[:], scale=2.0**40)
-        grouped2 = keep.tile([P, P * PACK], BF16, tag="group_sum", align_bytes=64)
+        nc.scalar.activation(inv_root[:], group_sum[:], ACT.Abs_reciprocal_sqrt, bias=guard[:], scale=ROOT_SCALE)
+        grouped2 = keep.tile([P, P * PACK], BF16, tag="group_sum", align_bytes=ALIGN)
         interleave_values(turned2, grouped2[:])
         turned3 = gather_values(3, "shares")
-        grouped3 = keep.tile([P, P * PACK], BF16, align_bytes=64)
+        grouped3 = keep.tile([P, P * PACK], BF16, align_bytes=ALIGN)
         interleave_values(turned3, grouped3[:])
-        factor = keep.tile([P, K, PACK], F32)
-        nc.vector.scalar_tensor_tensor(factor[:], inv_root[:], 2.0**20, os_cols[:].unsqueeze(1).to_broadcast([P, K, PACK]), ALU.mult, ALU.mult)
+        group_factor = keep.tile([P, K, PACK], F32)
+        nc.vector.scalar_tensor_tensor(
+            group_factor[:], inv_root[:], ROOT_UNDO, factor_cols[:].unsqueeze(1).to_broadcast([P, K, PACK]), ALU.mult, ALU.mult
+        )
 
-        v_codes = keep.tile([P, E], U32, tag="tiny", align_bytes=64)
-        v_scales = keep.tile([P, E], U8, align_bytes=64)
+        v_codes = keep.tile([P, E], U32, tag="guard", align_bytes=ALIGN)
+        v_scales = keep.tile([P, E], U8, align_bytes=ALIGN)
 
         def quantize_values(j, grouped):
             cols = slice(j * P, j * P + grouped.shape[1] // PACK)
             nc.vector.quantize_mx(out=v_codes[:, cols].bitcast(FP8X4), scales=v_scales[:, cols], in_=grouped)
 
         quantize_values(0, grouped01[:])
-        w_grouped = keep.tile([P, Q * PACK], BF16, align_bytes=64)
+        w_grouped = keep.tile([P, Q * PACK], BF16, align_bytes=ALIGN)
         nc.vector.tensor_tensor(
             w_grouped[:].rearrange("p (k j t) -> p k j t", j=GROUP, t=PACK),
             shares_t[:].rearrange("p (t k j) -> p k j t", t=PACK, j=GROUP),
-            factor[:].unsqueeze(2).to_broadcast([P, K, GROUP, PACK]),
+            group_factor[:].unsqueeze(2).to_broadcast([P, K, GROUP, PACK]),
             ALU.mult,
         )
         quantize_values(2, grouped2[:])
-        w_codes = keep.tile([P, Q], U32, align_bytes=64)
-        w_scales = keep.tile([P, Q], U8, align_bytes=64)
+        w_codes = keep.tile([P, Q], U32, align_bytes=ALIGN)
+        w_scales = keep.tile([P, Q], U8, align_bytes=ALIGN)
         nc.vector.quantize_mx(out=w_codes[:].bitcast(FP8X4), scales=w_scales[:], in_=w_grouped[:])
         quantize_values(3, grouped3[:])
 
-        for n, (c0, c1) in enumerate(((0, 256), (256, 384), (384, 512))):
+        for n, (c0, c1) in enumerate(OUT_PIECES):
             cols = slice(c0, c1)
-            acc = bank((6, 7, 4, 3)[n])
+            acc = bank(OUT_BANKS[n])
             nc.tensor.matmul_mx(
                 out=acc[:, 0 : c1 - c0],
                 lhsT=w_codes[:].bitcast(FP8X4),

from contextlib import ExitStack

import concourse.mybir as mybir
from concourse.masks import make_identity

D, T, I, Q, E, K = 512, 2048, 512, 128, 512, 16
FLOPS = 2 * Q * D * T + 2 * Q * I * E

F32 = mybir.dt.float32
BF16 = mybir.dt.bfloat16
I32 = mybir.dt.int32
U32 = mybir.dt.uint32
U16 = mybir.dt.uint16
U8 = mybir.dt.uint8
FP8X4 = mybir.dt.float8_e4m3fn_x4
ALU = mybir.AluOpType
ACT = mybir.ActivationFunctionType
AXIS = mybir.AxisListType

P = 128
PACK = 4
BANK = 512
GROUP = Q // K
LIST_ROWS = 16
QUADRANTS = 4
VALUE_TILES = E // P
ALIGN = 64

KEY_LOADS = ((0, 512), (512, 1024), (1024, 2048))
SCORE_PIECES = ((0, 512), (512, 1024), (1024, 1536), (1536, 1792), (1792, 2048))
SCALAR_SCORE_PIECE = 1
OUT_PIECES = ((0, 256), (256, 384), (384, 512))
SHARES_BANK = 5
OUT_BANKS = (6, 7, 4)
SLOT_HALVES = ((0, I // 2), (I // 2, I))
TOKEN_HALVES = ((0, T // 2), (T // 2, T))

ROOT_SCALE = 2.0**40
ROOT_UNDO = 2.0**20
GUARD_INVERSE_SQUARE = 2.0**96


def tile_attend_seconded_balanced_blend_kernel(tc, query, keys_words, keys_scales, lam, slot_factor, vals, before, hold, offs, offs2, offs3, out):
    nc = tc.nc
    with ExitStack() as ctx:
        lists = ctx.enter_context(tc.tile_pool(name="lists", bufs=1))
        keep = ctx.enter_context(tc.tile_pool(name="keep", bufs=1))
        psum = ctx.enter_context(tc.psum_pool(name="psum", bufs=1))

        def bank(b):
            return psum.tile([P, BANK], F32, name="bank%d" % b, tag="bank%d" % b)

        def entries(list_tile, first, last):
            return list_tile[:, first // LIST_ROWS : last // LIST_ROWS]

        key_scales = keep.tile([P, BANK], U8, align_bytes=ALIGN)
        nc.vector.memset(key_scales[:].bitcast(I32), 0)
        one = keep.tile([P, 1], F32)
        nc.vector.memset(one[:], 1.0)
        guard_source = keep.tile([P, 1], F32, tag="guard_source", align_bytes=ALIGN)
        nc.scalar.activation(guard_source[:], one[:], ACT.Copy, scale=GUARD_INVERSE_SQUARE)

        q_raw = keep.tile([P, PACK, Q], F32)
        nc.sync.dma_start(out=q_raw[:], in_=query.rearrange("(p t) q -> p t q", t=PACK))
        for quad in range(QUADRANTS):
            rows = keys_scales[0, 4 * quad : 4 * quad + 4, :].bitcast(I32)
            nc.sync.dma_start(
                out=key_scales[32 * quad : 32 * quad + 16, :].bitcast(I32),
                in_=rows.rearrange("r (j c) -> j r c", j=T // BANK),
            )
        key_rows = keys_words[0].rearrange("p n t -> p (n t)")
        key_tiles = []
        for n, (c0, c1) in enumerate(KEY_LOADS):
            words = keep.tile([P, c1 - c0], U32, name="keys%d" % n, align_bytes=ALIGN)
            nc.sync.dma_start(out=words[:].bitcast(I32), in_=key_rows[:, PACK * c0 : PACK * c1].bitcast(I32))
            key_tiles.append(words)
        own = lists.tile([P, I // LIST_ROWS], U16)
        seconder = lists.tile([P, I // LIST_ROWS], U16)
        opponent = lists.tile([P, I // LIST_ROWS], U16)
        val_tiles = [keep.tile([P, T], F32, name="vals%d" % j, tag="vals%d" % j, align_bytes=ALIGN) for j in range(VALUE_TILES)]
        lam_col = keep.tile([P, 1], F32)
        hold_col = keep.tile([P, 1], F32, tag="group_sum", align_bytes=ALIGN)
        factor_cols = keep.tile([P, PACK], F32)
        before_sb = keep.tile([P, E], F32)
        nc.sync.dma_start(out=val_tiles[0][:, 0 : T // 2], in_=vals[0:P, 0 : T // 2])
        nc.sync.dma_start(opponent[:], offs3)
        nc.sync.dma_start(seconder[:], offs2)
        nc.sync.dma_start(own[:], offs)
        nc.sync.dma_start(out=val_tiles[0][:, T // 2 : T], in_=vals[0:P, T // 2 : T])
        nc.sync.dma_start(out=before_sb[:], in_=before)
        nc.sync.dma_start(out=val_tiles[1][:], in_=vals[P : 2 * P, :])
        nc.sync.dma_start(out=lam_col[:], in_=lam)
        nc.sync.dma_start(out=val_tiles[2][:], in_=vals[2 * P : 3 * P, :])
        nc.sync.dma_start(out=hold_col[:], in_=hold)
        nc.sync.dma_start(out=val_tiles[3][:], in_=vals[3 * P : 4 * P, :])
        nc.sync.dma_start(out=factor_cols[:], in_=slot_factor.rearrange("o (p t) -> (o p) t", t=PACK))
        give = keep.tile([P, 1], F32)
        nc.gpsimd.tensor_scalar(give[:], hold_col[:], -1.0, 1.0, ALU.mult, ALU.add)
        stay = keep.tile([P, 1], F32)
        nc.gpsimd.tensor_copy(out=stay[:], in_=hold_col[:])

        ident = keep.tile([P, P], F32)
        make_identity(nc, ident[:])

        q_grouped = keep.tile([P, Q, PACK], BF16, align_bytes=ALIGN)
        nc.vector.tensor_copy(out=q_grouped[:], in_=q_raw[:].rearrange("p t q -> p q t"))
        q_codes = keep.tile([P, Q], U32, align_bytes=ALIGN)
        q_scales = keep.tile([P, Q], U8, align_bytes=ALIGN)
        nc.vector.quantize_mx(out=q_codes[:].bitcast(FP8X4), scales=q_scales[:], in_=q_grouped[:].rearrange("p q t -> p (q t)"))

        scores = keep.tile([P, T], F32)
        for n, (c0, c1) in enumerate(SCORE_PIECES):
            load = [m for m, (l0, l1) in enumerate(KEY_LOADS) if l0 <= c0 < l1][0]
            first = KEY_LOADS[load][0]
            plane = c0 // BANK
            acc = bank(n)
            nc.tensor.matmul_mx(
                out=acc[:, 0 : c1 - c0],
                lhsT=q_codes[:].bitcast(FP8X4),
                lhsT_scale=q_scales[:],
                rhs=key_tiles[load][:, c0 - first : c1 - first].bitcast(FP8X4),
                rhs_scale=key_scales[4 * plane : P, c0 - BANK * plane : c1 - BANK * plane],
                start=True,
                stop=True,
            )
            if n != SCALAR_SCORE_PIECE:
                nc.vector.tensor_copy(out=scores[:, c0:c1], in_=acc[:, 0 : c1 - c0])
            else:
                nc.scalar.copy(out=scores[:, c0:c1], in_=acc[:, 0 : c1 - c0])

        def turn_values(j, picked):
            pairs = picked[:].bitcast(F32)
            turned = bank(j)
            for u in range(2):
                nc.tensor.transpose(turned[:, u * P : (u + 1) * P], pairs[:, u : 2 * P : 2], ident[:])
            return turned

        def gather_values(j, tag):
            picked = keep.tile([P, I], BF16, name="picked%d" % j, tag=tag)
            nc.vector.tensor_copy(out=picked[:], in_=val_tiles[j][:].indirect(own[:]))
            return turn_values(j, picked)

        def interleave_values(turned, grouped):
            nc.scalar.copy(
                out=grouped.bitcast(F32).rearrange("p (e u) -> p e u", u=2),
                in_=turned[:, 0 : 2 * P].rearrange("p (u e) -> p e u", u=2),
            )

        rounded = keep.tile([P, T], BF16, tag="rounded")
        for c0, c1 in TOKEN_HALVES:
            nc.scalar.copy(out=rounded[:, c0:c1], in_=val_tiles[0][:, c0:c1])
        picked0 = keep.tile([P, I], BF16)
        half = I // 2
        nc.scalar.activation(picked0[:, 0:half], rounded[:].indirect(entries(own, 0, half)), ACT.Copy)

        against = keep.tile([P, I], F32)
        margin = keep.tile([P, I], F32)
        for i0, i1 in SLOT_HALVES:
            nc.vector.tensor_copy(out=against[:, i0:i1], in_=scores[:].indirect(entries(opponent, i0, i1)))
        for i0, i1 in SLOT_HALVES:
            nc.vector.tensor_tensor(margin[:, i0:i1], scores[:].indirect(entries(seconder, i0, i1)), against[:, i0:i1], ALU.subtract)
        direct = keep.tile([P, I], F32, tag="direct")
        for i0, i1 in SLOT_HALVES:
            nc.vector.tensor_copy(out=direct[:, i0:i1], in_=scores[:].indirect(entries(own, i0, i1)))
        vote = keep.tile([P, I], F32, tag="vals0", align_bytes=ALIGN)
        nc.scalar.activation(vote[:], margin[:], ACT.Tanh)
        nc.scalar.activation(picked0[:, half:I], rounded[:].indirect(entries(own, half, I)), ACT.Copy)
        turned0 = turn_values(0, picked0)
        kept = keep.tile([P, E], F32, tag="rounded")
        nc.scalar.activation(kept[:], before_sb[:], ACT.Copy, scale=stay[:])
        s = keep.tile([P, I], F32)
        for i0, i1 in SLOT_HALVES:
            nc.vector.scalar_tensor_tensor(s[:, i0:i1], vote[:, i0:i1], lam_col[:], direct[:, i0:i1], ALU.mult, ALU.add)

        neg_max = keep.tile([P, 1], F32)
        nc.vector.tensor_reduce(neg_max[:], s[:], AXIS.X, ALU.max, negate=True)
        p_dealt = keep.tile([P, I], F32, tag="p_dealt")
        row_sum = keep.tile([P, 1], F32, tag="row_sum")
        nc.scalar.activation(
            p_dealt[:].rearrange("q (t m) -> q m t", t=PACK),
            s[:].rearrange("q (m t) -> q m t", t=PACK),
            ACT.Exp,
            bias=neg_max[:],
            accum_out=row_sum[:],
        )
        guard = keep.tile([P, 1], F32, tag="guard", align_bytes=ALIGN)
        nc.scalar.activation(guard[:], p_dealt[:, 0:1], ACT.Abs_reciprocal_sqrt, bias=guard_source[:], scale=0.0)
        turned1 = gather_values(1, "direct")
        inv_sum = keep.tile([P, 1], F32)
        nc.vector.reciprocal(inv_sum[:], row_sum[:])
        shares = keep.tile([P, I], F32, tag="shares")
        nc.vector.tensor_scalar(shares[:], p_dealt[:], inv_sum[:], None, ALU.mult)
        shares_t = bank(SHARES_BANK)
        for t in range(PACK):
            nc.tensor.transpose(shares_t[:, t * P : (t + 1) * P], shares[:, t * P : (t + 1) * P], ident[:])
        grouped01 = keep.tile([P, 2 * P * PACK], BF16, tag="guard_source", align_bytes=ALIGN)
        interleave_values(turned0, grouped01[:, 0 : P * PACK])
        interleave_values(turned1, grouped01[:, P * PACK : 2 * P * PACK])
        turned2 = gather_values(2, "row_sum")

        group_sum = keep.tile([P, K, PACK], F32, tag="group_sum", align_bytes=ALIGN)
        nc.vector.tensor_reduce(
            group_sum[:].rearrange("p k t -> p t k"),
            shares_t[:].rearrange("p (t k j) -> p t k j", t=PACK, j=GROUP),
            AXIS.X,
            ALU.add,
        )
        inv_root = keep.tile([P, K, PACK], F32)
        nc.scalar.activation(inv_root[:], group_sum[:], ACT.Abs_reciprocal_sqrt, bias=guard[:], scale=ROOT_SCALE)
        grouped2 = keep.tile([P, P * PACK], BF16, tag="group_sum", align_bytes=ALIGN)
        interleave_values(turned2, grouped2[:])
        turned3 = gather_values(3, "shares")
        grouped3 = keep.tile([P, P * PACK], BF16, align_bytes=ALIGN)
        interleave_values(turned3, grouped3[:])
        group_factor = keep.tile([P, K, PACK], F32)
        nc.vector.scalar_tensor_tensor(
            group_factor[:], inv_root[:], ROOT_UNDO, factor_cols[:].unsqueeze(1).to_broadcast([P, K, PACK]), ALU.mult, ALU.mult
        )

        v_codes = keep.tile([P, E], U32, tag="guard", align_bytes=ALIGN)
        v_scales = keep.tile([P, E], U8, align_bytes=ALIGN)

        def quantize_values(j, grouped):
            cols = slice(j * P, j * P + grouped.shape[1] // PACK)
            nc.vector.quantize_mx(out=v_codes[:, cols].bitcast(FP8X4), scales=v_scales[:, cols], in_=grouped)

        quantize_values(0, grouped01[:])
        w_grouped = keep.tile([P, Q * PACK], BF16, align_bytes=ALIGN)
        nc.vector.tensor_tensor(
            w_grouped[:].rearrange("p (k j t) -> p k j t", j=GROUP, t=PACK),
            shares_t[:].rearrange("p (t k j) -> p k j t", t=PACK, j=GROUP),
            group_factor[:].unsqueeze(2).to_broadcast([P, K, GROUP, PACK]),
            ALU.mult,
        )
        quantize_values(2, grouped2[:])
        w_codes = keep.tile([P, Q], U32, align_bytes=ALIGN)
        w_scales = keep.tile([P, Q], U8, align_bytes=ALIGN)
        nc.vector.quantize_mx(out=w_codes[:].bitcast(FP8X4), scales=w_scales[:], in_=w_grouped[:])
        quantize_values(3, grouped3[:])

        for n, (c0, c1) in enumerate(OUT_PIECES):
            cols = slice(c0, c1)
            acc = bank(OUT_BANKS[n])
            nc.tensor.matmul_mx(
                out=acc[:, 0 : c1 - c0],
                lhsT=w_codes[:].bitcast(FP8X4),
                lhsT_scale=w_scales[:],
                rhs=v_codes[:, cols].bitcast(FP8X4),
                rhs_scale=v_scales[:, cols],
                start=True,
                stop=True,
            )
            result = keep.tile([P, c1 - c0], F32, name="result%d" % n)
            nc.vector.scalar_tensor_tensor(result[:], acc[:, 0 : c1 - c0], give[:], kept[:, cols], ALU.mult, ALU.add)
            (nc.sync if n % 2 == 0 else nc.scalar).dma_start(out=out[:, cols], in_=result[:])
